import numpy as np
import ml_dtypes


def mxq(x, axis, fmt="e4m3"):
    dtype, down = {"e4m3": (ml_dtypes.float8_e4m3fn, 7), "e5m2": (ml_dtypes.float8_e5m2, 14)}[fmt]
    v = np.moveaxis(np.asarray(x, np.float32).astype(ml_dtypes.bfloat16).astype(np.float64), axis, -1)
    blocks = v.reshape(v.shape[:-1] + (-1, 32))
    amax = np.abs(blocks).max(-1, keepdims=True)
    byte = np.maximum(np.where(amax > 0, np.frexp(amax)[1] - 1 + 127, 0) - down, 1)
    scale = np.exp2(byte - 127.0)
    codes = (blocks / scale).astype(np.float32).astype(dtype).astype(np.float64)
    return np.moveaxis((codes * scale).reshape(v.shape), -1, axis)


WIDE = False


def mx_kscale(k):
    if not WIDE:
        return np.ones(k)
    levels = np.array([10, -10, 5, -5, 0])
    if k % 512:
        return np.exp2(np.random.permutation(np.resize(levels, k // 32))).repeat(32)
    a = np.empty((k // 512, 16))
    for p in range(k // 512):
        a[p, :8] = np.random.permutation(np.resize(levels, 8))
        for g in range(8):
            far = levels[np.abs(levels - a[p, g]) >= 10]
            a[p, g + 8] = far[np.random.randint(len(far))]
    return np.exp2(a.ravel()).repeat(32)


def f64(x):
    return np.asarray(x).astype(np.float64)


def striped(idx):
    return np.tile(np.asarray(idx).reshape(-1, 16).T, (8, 1)).astype(np.uint16)


def unstriped(offs):
    return offs[:16].T.reshape(-1).astype(np.int64)


E2M1 = np.array([0.0, 0.5, 1.0, 1.5, 2.0, 3.0, 4.0, 6.0, -0.0, -0.5, -1.0, -1.5, -2.0, -3.0, -4.0, -6.0])


def pack_weight(w, fmt):
    k, n = w.shape
    w = f64(np.asarray(w, np.float32).astype(ml_dtypes.bfloat16)).reshape(k // 32, 32, n)
    amax = np.abs(w).max(1)
    if fmt == "e4m3":
        byte = np.frexp(amax)[1] - 1 + 127 - 7
    else:
        mant, ex = np.frexp(amax / 6.0)
        byte = np.where(mant > 0.5, ex, ex - 1) + 127
    byte = np.clip(np.where(amax > 0, byte, 1), 1, 254)
    scaled = (w * np.exp2(127.0 - byte)[:, None, :]).reshape(k, n).astype(np.float32)
    by_word = np.ascontiguousarray(scaled.reshape(k // 512, 128, 4, n).transpose(0, 1, 3, 2))
    if fmt == "e4m3":
        words = by_word.astype(ml_dtypes.float8_e4m3fn).view(np.uint8)
    else:
        c = by_word.astype(ml_dtypes.float4_e2m1fn).view(np.uint8) & 0xF
        words = (c[..., 0::2] | (c[..., 1::2] << 4)).reshape(k // 512, 128, 2 * n)
    return np.ascontiguousarray(words), np.ascontiguousarray(byte.astype(np.uint8).reshape(k // 512, 16, n))


def unpack_weight(words, scales, fmt):
    g, _, n = scales.shape
    words = np.ascontiguousarray(words).reshape(g, 128, n, -1)
    if fmt == "e4m3":
        vals = words.view(ml_dtypes.float8_e4m3fn).astype(np.float64)
    else:
        nib = np.empty((g, 128, n, 4), np.uint8)
        nib[..., 0::2] = words & 0xF
        nib[..., 1::2] = words >> 4
        vals = E2M1[nib]
    vals = vals * np.repeat(np.exp2(scales.astype(np.float64) - 127.0), 8, axis=1)[..., None]
    return vals.transpose(0, 1, 3, 2).reshape(g * 512, n)


D, T, I, Q, G = 512, 2048, 512, 1024, 64


def setup_inputs():
    n = np.random.standard_normal
    idx = np.random.permutation(T)[:I]
    fd = mx_kscale(D)
    keysp = pack_weight(n((D, T)) / fd[:, None], "e4m3")
    return {
        "query": (n((D, Q)) * 0.4 / np.sqrt(D) * fd[:, None]).astype(np.float32),
        "keys_words": keysp[0],
        "keys_scales": keysp[1],
        "offs": striped(idx),
    }


def reference(query, keys_words, keys_scales, offs):
    idx = unstriped(offs)
    keysu = unpack_weight(keys_words, keys_scales, "e4m3")
    queryq = mxq(f64(query), 0, "e4m3")
    keysidxg = keysu[:, idx]
    a = queryq.T @ keysidxg
    p = np.exp(a - np.max(a, axis=1, keepdims=True))
    w = p / np.sum(p, axis=1, keepdims=True)
    w1 = np.pad(w, ((0, 0), (1, 0)))[:, :I]
    w2 = np.pad(w, ((0, 0), (2, 0)))[:, :I]
    w3 = np.pad(w, ((0, 0), (3, 0)))[:, :I]
    w4 = np.pad(w, ((0, 0), (4, 0)))[:, :I]
    s = (w + w1 + w2 + w3 + w4) * 102.4
    st = s.T
    y = st.reshape(I, G, Q // G).sum(axis=2)
    return y

@@ -1,0 +1,184 @@
+from contextlib import ExitStack
+
+import concourse.mybir as mybir
+from concourse.masks import make_identity
+
+D, T, I, Q, G = 512, 2048, 512, 1024, 64
+FLOPS = 2 * D * I * Q
+
+F32 = mybir.dt.float32
+BF16 = mybir.dt.bfloat16
+I32 = mybir.dt.int32
+U32 = mybir.dt.uint32
+U16 = mybir.dt.uint16
+U8 = mybir.dt.uint8
+FP8X4 = mybir.dt.float8_e4m3fn_x4
+ACT = mybir.ActivationFunctionType
+ALU = mybir.AluOpType
+AX = mybir.AxisListType
+
+P = 128
+PACK = 4
+ROWS = Q // G
+PIECE = 256
+PAD = 8
+GAIN = 102.4
+GROUPS = (2, 2, 4)
+BATCHES = ((0,), (1,), (2, 3), (4, 5), (6, 7))
+
+
+def tile_attend_votes_kernel(tc, query, keys_words, keys_scales, offs, out):
+    nc = tc.nc
+    with ExitStack() as ctx:
+        keep = ctx.enter_context(tc.tile_pool(name="keep", bufs=1))
+        score_pool = ctx.enter_context(tc.psum_pool(name="scores", bufs=4))
+        vote_pool = ctx.enter_context(tc.psum_pool(name="votes", bufs=1))
+
+        offsets = keep.tile([P, I // 16], U16, name="offsets")
+        pool_words = keep.tile([P, T], U32, name="pool_words")
+        pool_scales = keep.tile([P, T], U8, name="pool_scales", tag="scales_then_words", align_bytes=64)
+        nc.gpsimd.memset(pool_scales[:].bitcast(I32), 0)
+        nc.sync.dma_start(offsets[:], offs)
+        nc.sync.dma_start(pool_words[:].bitcast(I32), keys_words[0].rearrange("p n t -> p (n t)").bitcast(I32))
+        for quad in range(4):
+            nc.scalar.dma_start(
+                pool_scales[32 * quad : 32 * quad + 4, :].bitcast(I32),
+                keys_scales[0, 4 * quad : 4 * quad + 4, :].bitcast(I32),
+            )
+        padded = []
+        for c in range(Q // PIECE):
+            zeros = keep.tile([P, PAD], F32, name=f"zeros{c}", tag=f"stage{c}")
+            nc.gpsimd.memset(zeros[:], 0.0)
+            if c <= len(GROUPS):
+                line = keep.tile([P, PAD + I], F32, name=f"line{c}")
+                nc.gpsimd.tensor_copy(line[:, 0:PAD], zeros[:])
+                padded.append(line)
+        sums = padded[: len(GROUPS)]
+        pairs = padded[len(GROUPS)]
+        raws = []
+        for c in range(Q // PIECE):
+            raw = keep.tile([P, PACK, PIECE], F32, name=f"raw{c}", tag=f"stage{c}")
+            nc.sync.dma_start(raw[:], query[:, c * PIECE : (c + 1) * PIECE].rearrange("(p t) q -> p t q", t=PACK))
+            raws.append(raw)
+
+        ident = keep.tile([P, P], F32, name="ident")
+        make_identity(nc, ident[:])
+        warm = keep.tile([P, 1], F32, name="warm")
+        nc.scalar.activation(warm[:], ident[:, 0:1], ACT.Exp)
+
+        key_scales = keep.tile([P, I], U8, name="key_scales", align_bytes=64)
+        nc.vector.tensor_copy(key_scales[:], pool_scales[:].indirect(offsets[:]))
+        key_words = keep.tile([P, I], U32, name="key_words", tag="scales_then_words", align_bytes=64)
+        nc.vector.tensor_copy(key_words[:], pool_words[:].indirect(offsets[:]))
+
+        tiles = []
+        first = 0
+        for grp, n in enumerate(GROUPS):
+            for r in range(n):
+                tiles.append((grp, n, r, first))
+            first = first + n
+
+        operands = {}
+        banks = {}
+        stats = {}
+        probs = {}
+
+        def quantise(batch):
+            width = len(batch) * P
+            woven = keep.tile([P, width * PACK], BF16, name=f"woven{batch[0]}", align_bytes=64)
+            for place, k in enumerate(batch):
+                grp, n, r, first = tiles[k]
+                pieces = n * P // PIECE
+                parts = 1
+                quads = 32 // pieces // parts
+                for h in range(pieces * parts):
+                    raw = raws[first * P // PIECE + h // parts]
+                    u0 = (h % parts) * quads
+                    src = raw[:].rearrange("p t (u r j) -> p r u t j", r=n, j=4)[:, r, u0 : u0 + quads]
+                    c0 = place * P * PACK + 16 * quads * h
+                    dst = woven[:, c0 : c0 + 16 * quads].rearrange("p (u j t) -> p u t j", j=4, t=PACK)
+                    if (k, h) in ():
+                        nc.vector.tensor_copy(dst, src)
+                    else:
+                        nc.scalar.copy(dst, src)
+            codes = keep.tile([P, width], U32, name=f"codes{batch[0]}", align_bytes=64)
+            scales = keep.tile([P, width], U8, name=f"scales{batch[0]}", align_bytes=64)
+            nc.vector.quantize_mx(out=codes[:].bitcast(FP8X4), scales=scales[:], in_=woven[:])
+            for place, k in enumerate(batch):
+                operands[k] = (codes[:, place * P : (place + 1) * P], scales[:, place * P : (place + 1) * P])
+
+        def score(k):
+            codes, scales = operands[k]
+            bank = score_pool.tile([P, I], F32, name="score")
+            nc.tensor.matmul_mx(
+                out=bank[:], lhsT=codes.bitcast(FP8X4), lhsT_scale=scales,
+                rhs=key_words[:].bitcast(FP8X4), rhs_scale=key_scales[:], start=True, stop=True,
+            )
+            banks[k] = bank
+
+        def weigh(k):
+            neg_max = keep.tile([P, 1], F32, name=f"neg_max{k}")
+            nc.vector.tensor_reduce(neg_max[:], banks[k][:], AX.X, ALU.max, negate=True)
+            prob = keep.tile([P, I], F32, name=f"prob{k}")
+            total = keep.tile([P, 1], F32, name=f"total{k}")
+            nc.scalar.activation(prob[:], banks[k][:], ACT.Exp, bias=neg_max[:], accum_out=total[:])
+            probs[k] = prob
+            stats[k] = total
+
+        def gather_votes(grp, n, first, b0, nb, terms, queue):
+            heads = n * P // ROWS
+            bank = vote_pool.tile([P, nb, P], F32, name=f"vote{grp}_{b0}")
+            for b in range(nb):
+                for s, (src, back) in enumerate(terms):
+                    c0 = PAD + (b0 + b) * P - back
+                    nc.tensor.matmul(
+                        bank[:, b, :], src[:, c0 : c0 + P], ident[:],
+                        start=(s == 0), stop=(s == len(terms) - 1), is_transpose=True,
+                    )
+            summed = keep.tile([P, nb, heads], F32, name=f"summed{grp}_{b0}")
+            nc.vector.tensor_reduce(summed[:], bank[:].rearrange("p b (g j) -> p b g j", g=heads), AX.X, ALU.add)
+            votes = keep.tile([P, nb, heads], F32, name=f"votes{grp}_{b0}")
+            nc.scalar.mul(votes[:], summed[:], GAIN)
+            g0 = first * P // ROWS
+            queue.dma_start(
+                out[b0 * P : (b0 + nb) * P, g0 : g0 + heads].rearrange("(b p) g -> p b g", p=P), votes[:]
+            )
+
+        def add_up(k):
+            grp, n, r, first = tiles[k]
+            acc = sums[grp]
+            inv = keep.tile([P, 1], F32, name=f"inv{k}")
+            nc.vector.reciprocal(inv[:], stats[k][:])
+            if r == 0:
+                nc.scalar.activation(acc[:, PAD:], probs[k][:], ACT.Copy, scale=inv[:])
+            elif k < len(tiles) - 1:
+                nc.vector.scalar_tensor_tensor(acc[:, PAD:], probs[k][:], inv[:], acc[:, PAD:], ALU.mult, ALU.add)
+            if k == len(tiles) - 1:
+                half = I // 2
+                for h in range(2):
+                    c0 = PAD + h * half
+                    nc.vector.scalar_tensor_tensor(
+                        acc[:, c0 : c0 + half], probs[k][:, h * half : (h + 1) * half], inv[:],
+                        acc[:, c0 : c0 + half], ALU.mult, ALU.add,
+                    )
+                for h in range(2):
+                    c0 = PAD + h * half
+                    nc.vector.tensor_tensor(
+                        pairs[:, c0 : c0 + half], acc[:, c0 : c0 + half], acc[:, c0 - 1 : c0 - 1 + half], ALU.add
+                    )
+                for h in range(2):
+                    gather_votes(grp, n, first, 2 * h, 2, [(acc, 4), (pairs, 0), (pairs, 2)], nc.sync)
+
+        for step in range(len(tiles) + 2):
+            for batch in BATCHES:
+                if batch[0] == step + 1 or (step == 0 and batch[0] < 1):
+                    quantise(batch)
+            if step < len(tiles):
+                score(step)
+            if 0 <= step - 1 < len(tiles):
+                weigh(step - 1)
+            if 0 <= step - 2:
+                add_up(step - 2)
+        for grp, n, r, first in tiles[:-1]:
+            if r == n - 1:
+                gather_votes(grp, n, first, 0, 4, [(sums[grp], back) for back in range(5)], nc.sync)

@@ -1,7 +1,6 @@
 from contextlib import ExitStack
 
 import concourse.mybir as mybir
-from concourse.masks import make_identity
 
 D, T, I, Q, G = 512, 2048, 512, 1024, 64
 FLOPS = 2 * D * I * Q
@@ -20,11 +19,13 @@ AX = mybir.AxisListType
 P = 128
 PACK = 4
 ROWS = Q // G
+BLOCKS = I // P
+HALF_HEADS = G // 2
+WINDOW = 5
 PIECE = 256
-PAD = 8
 GAIN = 102.4
 GROUPS = (2, 2, 4)
-BATCHES = ((0,), (1,), (2, 3), (4, 5), (6, 7))
+BATCHES = ((0, 1), (2, 3), (4, 5), (6, 7))
 
 
 def tile_attend_votes_kernel(tc, query, keys_words, keys_scales, offs, out):
@@ -32,73 +33,76 @@ def tile_attend_votes_kernel(tc, query, keys_words, keys_scales, offs, out):
     with ExitStack() as ctx:
         keep = ctx.enter_context(tc.tile_pool(name="keep", bufs=1))
         score_pool = ctx.enter_context(tc.psum_pool(name="scores", bufs=4))
-        vote_pool = ctx.enter_context(tc.psum_pool(name="votes", bufs=1))
+        sum_pool = ctx.enter_context(tc.psum_pool(name="sums", bufs=3))
+        turn_pool = ctx.enter_context(tc.psum_pool(name="turns", bufs=1))
+
+        firsts = [sum(GROUPS[:grp]) for grp in range(len(GROUPS))]
+
+        def load_piece(c):
+            raw = keep.tile([P, PACK, PIECE], F32, name=f"raw{c}", tag=f"stage{c}")
+            nc.sync.dma_start(raw[:], query[:, c * PIECE : (c + 1) * PIECE].rearrange("(p t) q -> p t q", t=PACK))
+            return raw
 
         offsets = keep.tile([P, I // 16], U16, name="offsets")
-        pool_words = keep.tile([P, T], U32, name="pool_words")
         pool_scales = keep.tile([P, T], U8, name="pool_scales", tag="scales_then_words", align_bytes=64)
         nc.gpsimd.memset(pool_scales[:].bitcast(I32), 0)
+        raws = [load_piece(0)]
         nc.sync.dma_start(offsets[:], offs)
-        nc.sync.dma_start(pool_words[:].bitcast(I32), keys_words[0].rearrange("p n t -> p (n t)").bitcast(I32))
         for quad in range(4):
-            nc.scalar.dma_start(
+            nc.sync.dma_start(
                 pool_scales[32 * quad : 32 * quad + 4, :].bitcast(I32),
                 keys_scales[0, 4 * quad : 4 * quad + 4, :].bitcast(I32),
             )
-        padded = []
-        for c in range(Q // PIECE):
-            zeros = keep.tile([P, PAD], F32, name=f"zeros{c}", tag=f"stage{c}")
+        head_sums = []
+        for half, tag in enumerate(("stage_words", "stage1")):
+            zeros = keep.tile([P, HALF_HEADS], F32, name=f"zeros{half}", tag=tag)
             nc.gpsimd.memset(zeros[:], 0.0)
-            if c <= len(GROUPS):
-                line = keep.tile([P, PAD + I], F32, name=f"line{c}")
-                nc.gpsimd.tensor_copy(line[:, 0:PAD], zeros[:])
-                padded.append(line)
-        sums = padded[: len(GROUPS)]
-        pairs = padded[len(GROUPS)]
-        raws = []
-        for c in range(Q // PIECE):
-            raw = keep.tile([P, PACK, PIECE], F32, name=f"raw{c}", tag=f"stage{c}")
-            nc.sync.dma_start(raw[:], query[:, c * PIECE : (c + 1) * PIECE].rearrange("(p t) q -> p t q", t=PACK))
-            raws.append(raw)
-
+            sums = keep.tile([P, (BLOCKS + 1) * HALF_HEADS], F32, name=f"head_sums{half}")
+            nc.gpsimd.tensor_copy(sums[:, 0:HALF_HEADS], zeros[:])
+            head_sums.append(sums)
+        zeros = keep.tile([P, P], F32, name="zeros_square", tag="stage2")
+        nc.gpsimd.memset(zeros[:], 0.0)
         ident = keep.tile([P, P], F32, name="ident")
-        make_identity(nc, ident[:])
+        nc.gpsimd.affine_select(
+            out=ident[:], in_=zeros[:], compare_op=ALU.not_equal, fill=1.0, base=0,
+            pattern=[[-1, P]], channel_multiplier=1,
+        )
+        pool_words = keep.tile([P, T], U32, name="pool_words", tag="stage_words")
+        nc.sync.dma_start(pool_words[:].bitcast(I32), keys_words[0].rearrange("p n t -> p (n t)").bitcast(I32))
+        zeros = keep.tile([P, 1], F32, name="zeros_column", tag="stage3")
+        nc.gpsimd.memset(zeros[:], 0.0)
         warm = keep.tile([P, 1], F32, name="warm")
-        nc.scalar.activation(warm[:], ident[:, 0:1], ACT.Exp)
-
-        key_scales = keep.tile([P, I], U8, name="key_scales", align_bytes=64)
-        nc.vector.tensor_copy(key_scales[:], pool_scales[:].indirect(offsets[:]))
-        key_words = keep.tile([P, I], U32, name="key_words", tag="scales_then_words", align_bytes=64)
-        nc.vector.tensor_copy(key_words[:], pool_words[:].indirect(offsets[:]))
+        nc.scalar.activation(warm[:], zeros[:], ACT.Exp)
+        for c in range(1, Q // PIECE):
+            raws.append(load_piece(c))
 
         tiles = []
-        first = 0
         for grp, n in enumerate(GROUPS):
             for r in range(n):
-                tiles.append((grp, n, r, first))
-            first = first + n
+                tiles.append((grp, n, r))
 
         operands = {}
         banks = {}
         stats = {}
         probs = {}
+        sum_banks = {}
 
         def quantise(batch):
             width = len(batch) * P
             woven = keep.tile([P, width * PACK], BF16, name=f"woven{batch[0]}", align_bytes=64)
             for place, k in enumerate(batch):
-                grp, n, r, first = tiles[k]
+                grp, n, r = tiles[k]
                 pieces = n * P // PIECE
-                parts = 1
-                quads = 32 // pieces // parts
-                for h in range(pieces * parts):
-                    raw = raws[first * P // PIECE + h // parts]
-                    u0 = (h % parts) * quads
-                    src = raw[:].rearrange("p t (u r j) -> p r u t j", r=n, j=4)[:, r, u0 : u0 + quads]
-                    c0 = place * P * PACK + 16 * quads * h
-                    dst = woven[:, c0 : c0 + 16 * quads].rearrange("p (u j t) -> p u t j", j=4, t=PACK)
-                    if (k, h) in ():
+                for h in range(pieces):
+                    src = raws[firsts[grp] * P // PIECE + h][:].rearrange("p t (u r j) -> p r u t j", r=n, j=4)[:, r]
+                    c0 = place * P * PACK + h * P * PACK // pieces
+                    dst = woven[:, c0 : c0 + P * PACK // pieces].rearrange("p (u j t) -> p u t j", j=4, t=PACK)
+                    if (k, h) in ((0, 0),):
                         nc.vector.tensor_copy(dst, src)
+                    elif (k, h) in ((2, 0), (4, 0), (5, 0), (6, 0)):
+                        nc.gpsimd.tensor_scalar(
+                            dst.rearrange("p u t j -> p u j t"), src.rearrange("p u t j -> p u j t"), 1.0, 0.0, ALU.mult, ALU.add
+                        )
                     else:
                         nc.scalar.copy(dst, src)
             codes = keep.tile([P, width], U32, name=f"codes{batch[0]}", align_bytes=64)
@@ -106,6 +110,12 @@ def tile_attend_votes_kernel(tc, query, keys_words, keys_scales, offs, out):
             nc.vector.quantize_mx(out=codes[:].bitcast(FP8X4), scales=scales[:], in_=woven[:])
             for place, k in enumerate(batch):
                 operands[k] = (codes[:, place * P : (place + 1) * P], scales[:, place * P : (place + 1) * P])
+
+        quantise(BATCHES[0])
+        key_scales = keep.tile([P, I], U8, name="key_scales", align_bytes=64)
+        nc.vector.tensor_copy(key_scales[:], pool_scales[:].indirect(offsets[:]))
+        key_words = keep.tile([P, I], U32, name="key_words", tag="scales_then_words", align_bytes=64)
+        nc.vector.tensor_copy(key_words[:], pool_words[:].indirect(offsets[:]))
 
         def score(k):
             codes, scales = operands[k]
@@ -125,60 +135,71 @@ def tile_attend_votes_kernel(tc, query, keys_words, keys_scales, offs, out):
             probs[k] = prob
             stats[k] = total
 
-        def gather_votes(grp, n, first, b0, nb, terms, queue):
-            heads = n * P // ROWS
-            bank = vote_pool.tile([P, nb, P], F32, name=f"vote{grp}_{b0}")
-            for b in range(nb):
-                for s, (src, back) in enumerate(terms):
-                    c0 = PAD + (b0 + b) * P - back
-                    nc.tensor.matmul(
-                        bank[:, b, :], src[:, c0 : c0 + P], ident[:],
-                        start=(s == 0), stop=(s == len(terms) - 1), is_transpose=True,
-                    )
-            summed = keep.tile([P, nb, heads], F32, name=f"summed{grp}_{b0}")
-            nc.vector.tensor_reduce(summed[:], bank[:].rearrange("p b (g j) -> p b g j", g=heads), AX.X, ALU.add)
-            votes = keep.tile([P, nb, heads], F32, name=f"votes{grp}_{b0}")
-            nc.scalar.mul(votes[:], summed[:], GAIN)
-            g0 = first * P // ROWS
-            queue.dma_start(
-                out[b0 * P : (b0 + nb) * P, g0 : g0 + heads].rearrange("(b p) g -> p b g", p=P), votes[:]
-            )
-
         def add_up(k):
-            grp, n, r, first = tiles[k]
-            acc = sums[grp]
+            grp, n, r = tiles[k]
+            parts = n // 2
+            blocks = BLOCKS // parts
+            if r == 0:
+                sum_banks[grp] = [sum_pool.tile([P, blocks, P], F32, name="sum_bank") for part in range(parts)]
             inv = keep.tile([P, 1], F32, name=f"inv{k}")
             nc.vector.reciprocal(inv[:], stats[k][:])
-            if r == 0:
-                nc.scalar.activation(acc[:, PAD:], probs[k][:], ACT.Copy, scale=inv[:])
-            elif k < len(tiles) - 1:
-                nc.vector.scalar_tensor_tensor(acc[:, PAD:], probs[k][:], inv[:], acc[:, PAD:], ALU.mult, ALU.add)
-            if k == len(tiles) - 1:
-                half = I // 2
+            weights = keep.tile([P, I], F32, name=f"weights{k}")
+            if k in (5, 6, 7):
                 for h in range(2):
-                    c0 = PAD + h * half
-                    nc.vector.scalar_tensor_tensor(
-                        acc[:, c0 : c0 + half], probs[k][:, h * half : (h + 1) * half], inv[:],
-                        acc[:, c0 : c0 + half], ALU.mult, ALU.add,
-                    )
-                for h in range(2):
-                    c0 = PAD + h * half
-                    nc.vector.tensor_tensor(
-                        pairs[:, c0 : c0 + half], acc[:, c0 : c0 + half], acc[:, c0 - 1 : c0 - 1 + half], ALU.add
-                    )
-                for h in range(2):
-                    gather_votes(grp, n, first, 2 * h, 2, [(acc, 4), (pairs, 0), (pairs, 2)], nc.sync)
+                    cols = slice(h * I // 2, (h + 1) * I // 2)
+                    nc.vector.tensor_scalar(weights[:, cols], probs[k][:, cols], inv[:], GAIN, ALU.mult, ALU.mult)
+            else:
+                nc.gpsimd.tensor_scalar(weights[:], probs[k][:], inv[:], GAIN, ALU.mult, ALU.mult)
+            for b in range(BLOCKS):
+                nc.tensor.matmul(
+                    sum_banks[grp][b // blocks][:, b % blocks, :], weights[:, b * P : (b + 1) * P], ident[:],
+                    start=(r == 0 and b % blocks == 0), stop=(r == n - 1 and b % blocks == blocks - 1),
+                    is_transpose=True,
+                )
+
+        def sum_heads(grp):
+            heads = GROUPS[grp] * P // ROWS
+            half, g0 = divmod(firsts[grp] * P // ROWS, HALF_HEADS)
+            by_block = head_sums[half][:, HALF_HEADS:].rearrange("p (b g) -> p b g", g=HALF_HEADS)
+            blocks = BLOCKS // len(sum_banks[grp])
+            for part, bank in enumerate(sum_banks[grp]):
+                nc.vector.tensor_reduce(
+                    by_block[:, part * blocks : (part + 1) * blocks, g0 : g0 + heads],
+                    bank[:].rearrange("p b (g j) -> p b g j", g=heads), AX.X, ALU.add,
+                )
+
+        def smooth(half):
+            back = turn_pool.tile([P, 2 * P], F32, name="turn")
+            for s in range(2):
+                nc.tensor.transpose(back[:, s * P : (s + 1) * P], head_sums[half][:, s * HALF_HEADS : s * HALF_HEADS + P], ident[:])
+            reach = WINDOW - 1
+            line = keep.tile([P, P + reach], F32, name=f"line{half}")
+            nc.scalar.copy(line[:], back[:, P - reach :])
+            forth = turn_pool.tile([P, P], F32, name="turn")
+            for s in range(WINDOW):
+                nc.tensor.matmul(
+                    forth[:], line[:, s : s + P], ident[:], start=(s == 0), stop=(s == WINDOW - 1), is_transpose=True
+                )
+            votes = keep.tile([P, BLOCKS, HALF_HEADS], F32, name=f"votes{half}")
+            nc.scalar.copy(votes[:].rearrange("p b g -> p (b g)"), forth[:])
+            nc.sync.dma_start(
+                out[:, half * HALF_HEADS : (half + 1) * HALF_HEADS].rearrange("(b p) g -> p b g", p=P), votes[:]
+            )
 
         for step in range(len(tiles) + 2):
-            for batch in BATCHES:
-                if batch[0] == step + 1 or (step == 0 and batch[0] < 1):
+            for batch in BATCHES[1:]:
+                if batch[0] == step + 2:
                     quantise(batch)
             if step < len(tiles):
                 score(step)
             if 0 <= step - 1 < len(tiles):
                 weigh(step - 1)
+            if step == 5:
+                sum_heads(0)
+            if step == 7:
+                sum_heads(1)
+                smooth(0)
             if 0 <= step - 2:
                 add_up(step - 2)
-        for grp, n, r, first in tiles[:-1]:
-            if r == n - 1:
-                gather_votes(grp, n, first, 0, 4, [(sums[grp], back) for back in range(5)], nc.sync)
+        sum_heads(2)
+        smooth(1)

@@ -18,35 +18,34 @@ AX = mybir.AxisListType
 
 P = 128
 PACK = 4
-ROWS = Q // G
+RUN = 4
+PAIR = 2
+GROUP_ROWS = PAIR * P
+GROUPS = Q // GROUP_ROWS
+TILES = Q // P
+GROUP_HEADS = G // GROUPS
 BLOCKS = I // P
 HALF_HEADS = G // 2
 WINDOW = 5
-PIECE = 256
 GAIN = 102.4
-GROUPS = (2, 2, 4)
-BATCHES = ((0, 1), (2, 3), (4, 5), (6, 7))
 
 
 def tile_attend_votes_kernel(tc, query, keys_words, keys_scales, offs, out):
     nc = tc.nc
     with ExitStack() as ctx:
         keep = ctx.enter_context(tc.tile_pool(name="keep", bufs=1))
-        score_pool = ctx.enter_context(tc.psum_pool(name="scores", bufs=4))
-        sum_pool = ctx.enter_context(tc.psum_pool(name="sums", bufs=3))
-        turn_pool = ctx.enter_context(tc.psum_pool(name="turns", bufs=1))
+        psum = ctx.enter_context(tc.psum_pool(name="psum", bufs=1))
 
-        firsts = [sum(GROUPS[:grp]) for grp in range(len(GROUPS))]
-
-        def load_piece(c):
-            raw = keep.tile([P, PACK, PIECE], F32, name=f"raw{c}", tag=f"stage{c}")
-            nc.sync.dma_start(raw[:], query[:, c * PIECE : (c + 1) * PIECE].rearrange("(p t) q -> p t q", t=PACK))
+        def load_group(grp):
+            raw = keep.tile([P, PACK, GROUP_ROWS], F32, name=f"raw{grp}", tag=f"raw{grp}")
+            rows = query[:, grp * GROUP_ROWS : (grp + 1) * GROUP_ROWS]
+            nc.sync.dma_start(raw[:], rows.rearrange("(p t) q -> p t q", t=PACK))
             return raw
 
         offsets = keep.tile([P, I // 16], U16, name="offsets")
         pool_scales = keep.tile([P, T], U8, name="pool_scales", tag="scales_then_words", align_bytes=64)
         nc.gpsimd.memset(pool_scales[:].bitcast(I32), 0)
-        raws = [load_piece(0)]
+        raws = [load_group(0)]
         nc.sync.dma_start(offsets[:], offs)
         for quad in range(4):
             nc.sync.dma_start(
@@ -54,152 +53,152 @@ def tile_attend_votes_kernel(tc, query, keys_words, keys_scales, offs, out):
                 keys_scales[0, 4 * quad : 4 * quad + 4, :].bitcast(I32),
             )
         head_sums = []
-        for half, tag in enumerate(("stage_words", "stage1")):
+        for half, tag in enumerate(("pool_words", "raw1")):
             zeros = keep.tile([P, HALF_HEADS], F32, name=f"zeros{half}", tag=tag)
             nc.gpsimd.memset(zeros[:], 0.0)
             sums = keep.tile([P, (BLOCKS + 1) * HALF_HEADS], F32, name=f"head_sums{half}")
             nc.gpsimd.tensor_copy(sums[:, 0:HALF_HEADS], zeros[:])
             head_sums.append(sums)
-        zeros = keep.tile([P, P], F32, name="zeros_square", tag="stage2")
-        nc.gpsimd.memset(zeros[:], 0.0)
+        zero_square = keep.tile([P, P], F32, name="zero_square", tag="raw2")
+        nc.gpsimd.memset(zero_square[:], 0.0)
+        one_square = keep.tile([P, P], F32, name="one_square", tag="raw3")
+        nc.scalar.activation(one_square[:], zero_square[:], ACT.Exp)
         ident = keep.tile([P, P], F32, name="ident")
         nc.gpsimd.affine_select(
-            out=ident[:], in_=zeros[:], compare_op=ALU.not_equal, fill=1.0, base=0,
+            out=ident[:], in_=one_square[:], compare_op=ALU.is_equal, fill=0.0, base=0,
             pattern=[[-1, P]], channel_multiplier=1,
         )
-        pool_words = keep.tile([P, T], U32, name="pool_words", tag="stage_words")
+        pool_words = keep.tile([P, T], U32, name="pool_words", tag="pool_words")
         nc.sync.dma_start(pool_words[:].bitcast(I32), keys_words[0].rearrange("p n t -> p (n t)").bitcast(I32))
-        zeros = keep.tile([P, 1], F32, name="zeros_column", tag="stage3")
-        nc.gpsimd.memset(zeros[:], 0.0)
-        warm = keep.tile([P, 1], F32, name="warm")
-        nc.scalar.activation(warm[:], zeros[:], ACT.Exp)
-        for c in range(1, Q // PIECE):
-            raws.append(load_piece(c))
-
-        tiles = []
-        for grp, n in enumerate(GROUPS):
-            for r in range(n):
-                tiles.append((grp, n, r))
+        for grp in range(1, GROUPS):
+            raws.append(load_group(grp))
 
         operands = {}
-        banks = {}
-        stats = {}
+        scores = {}
+        totals = {}
         probs = {}
+        weights = {}
         sum_banks = {}
 
-        def quantise(batch):
-            width = len(batch) * P
-            woven = keep.tile([P, width * PACK], BF16, name=f"woven{batch[0]}", align_bytes=64)
-            for place, k in enumerate(batch):
-                grp, n, r = tiles[k]
-                pieces = n * P // PIECE
-                for h in range(pieces):
-                    src = raws[firsts[grp] * P // PIECE + h][:].rearrange("p t (u r j) -> p r u t j", r=n, j=4)[:, r]
-                    c0 = place * P * PACK + h * P * PACK // pieces
-                    dst = woven[:, c0 : c0 + P * PACK // pieces].rearrange("p (u j t) -> p u t j", j=4, t=PACK)
-                    if (k, h) in ((0, 0),):
-                        nc.vector.tensor_copy(dst, src)
-                    elif (k, h) in ((2, 0), (4, 0), (5, 0), (6, 0)):
-                        nc.gpsimd.tensor_scalar(
-                            dst.rearrange("p u t j -> p u j t"), src.rearrange("p u t j -> p u j t"), 1.0, 0.0, ALU.mult, ALU.add
-                        )
-                    else:
-                        nc.scalar.copy(dst, src)
-            codes = keep.tile([P, width], U32, name=f"codes{batch[0]}", align_bytes=64)
-            scales = keep.tile([P, width], U8, name=f"scales{batch[0]}", align_bytes=64)
+        def quantise(grp):
+            woven = keep.tile([P, GROUP_ROWS * PACK], BF16, name=f"woven{grp}", tag=f"woven{grp}", align_bytes=64)
+            src = raws[grp][:].rearrange("p t (u r j) -> p r u t j", r=PAIR, j=RUN)
+            dst = woven[:].rearrange("p (r u j t) -> p r u t j", r=PAIR, j=RUN, t=PACK)
+            if grp == 0:
+                nc.vector.tensor_copy(dst[:, 0], src[:, 0])
+                nc.scalar.copy(dst[:, 1], src[:, 1])
+            elif grp % 2 == 0:
+                nc.vector.tensor_copy(dst, src)
+            else:
+                nc.scalar.copy(dst, src)
+            codes = keep.tile([P, GROUP_ROWS], U32, name=f"codes{grp}", align_bytes=64)
+            scales = keep.tile([P, GROUP_ROWS], U8, name=f"scales{grp}", align_bytes=64)
             nc.vector.quantize_mx(out=codes[:].bitcast(FP8X4), scales=scales[:], in_=woven[:])
-            for place, k in enumerate(batch):
-                operands[k] = (codes[:, place * P : (place + 1) * P], scales[:, place * P : (place + 1) * P])
+            operands[grp] = (codes, scales)
 
-        quantise(BATCHES[0])
+        quantise(0)
         key_scales = keep.tile([P, I], U8, name="key_scales", align_bytes=64)
         nc.vector.tensor_copy(key_scales[:], pool_scales[:].indirect(offsets[:]))
         key_words = keep.tile([P, I], U32, name="key_words", tag="scales_then_words", align_bytes=64)
-        nc.vector.tensor_copy(key_words[:], pool_words[:].indirect(offsets[:]))
+        for h in range(2):
+            nc.vector.tensor_copy(
+                key_words[:, h * I // 2 : (h + 1) * I // 2],
+                pool_words[:].indirect(offsets[:, h * I // 32 : (h + 1) * I // 32]),
+            )
 
         def score(k):
-            codes, scales = operands[k]
-            bank = score_pool.tile([P, I], F32, name="score")
-            nc.tensor.matmul_mx(
-                out=bank[:], lhsT=codes.bitcast(FP8X4), lhsT_scale=scales,
-                rhs=key_words[:].bitcast(FP8X4), rhs_scale=key_scales[:], start=True, stop=True,
-            )
-            banks[k] = bank
+            codes, scales = operands[k // PAIR]
+            rows = slice(k % PAIR * P, (k % PAIR + 1) * P)
+            scores[k] = psum.tile([P, I], F32, name=f"scores{k}", tag=f"bank{k}")
+            cuts = 2 if k == 0 else 1
+            for h in range(cuts):
+                cols = slice(h * I // cuts, (h + 1) * I // cuts)
+                nc.tensor.matmul_mx(
+                    out=scores[k][:, cols], lhsT=codes[:, rows].bitcast(FP8X4), lhsT_scale=scales[:, rows],
+                    rhs=key_words[:, cols].bitcast(FP8X4), rhs_scale=key_scales[:, cols], start=True, stop=True,
+                )
 
-        def weigh(k):
-            neg_max = keep.tile([P, 1], F32, name=f"neg_max{k}")
-            nc.vector.tensor_reduce(neg_max[:], banks[k][:], AX.X, ALU.max, negate=True)
-            prob = keep.tile([P, I], F32, name=f"prob{k}")
-            total = keep.tile([P, 1], F32, name=f"total{k}")
-            nc.scalar.activation(prob[:], banks[k][:], ACT.Exp, bias=neg_max[:], accum_out=total[:])
-            probs[k] = prob
-            stats[k] = total
+        def exponentiate(k):
+            tag = "woven1" if k == 1 else f"neg_max{k}"
+            neg_max = keep.tile([P, 1], F32, name=f"neg_max{k}", tag=tag, align_bytes=64)
+            nc.vector.tensor_reduce(neg_max[:], scores[k][:], AX.X, ALU.max, negate=True)
+            probs[k] = keep.tile([P, I], F32, name=f"probs{k}")
+            totals[k] = keep.tile([P, 1], F32, name=f"totals{k}")
+            nc.scalar.activation(probs[k][:], scores[k][:], ACT.Exp, bias=neg_max[:], accum_out=totals[k][:])
 
-        def add_up(k):
-            grp, n, r = tiles[k]
-            parts = n // 2
-            blocks = BLOCKS // parts
-            if r == 0:
-                sum_banks[grp] = [sum_pool.tile([P, blocks, P], F32, name="sum_bank") for part in range(parts)]
+        def normalise(k):
             inv = keep.tile([P, 1], F32, name=f"inv{k}")
-            nc.vector.reciprocal(inv[:], stats[k][:])
-            weights = keep.tile([P, I], F32, name=f"weights{k}")
-            if k in (5, 6, 7):
-                for h in range(2):
-                    cols = slice(h * I // 2, (h + 1) * I // 2)
-                    nc.vector.tensor_scalar(weights[:, cols], probs[k][:, cols], inv[:], GAIN, ALU.mult, ALU.mult)
+            nc.vector.reciprocal(inv[:], totals[k][:])
+            weights[k] = keep.tile([P, I], F32, name=f"weights{k}")
+            if k < TILES // 2:
+                nc.gpsimd.tensor_scalar(weights[k][:], probs[k][:], inv[:], 1.0, ALU.mult, ALU.mult)
+            elif k == TILES - 1:
+                nc.scalar.activation(weights[k][:, : I // 2], probs[k][:, : I // 2], ACT.Copy, scale=inv[:])
+                nc.vector.tensor_scalar_mul(weights[k][:, I // 2 :], probs[k][:, I // 2 :], inv[:])
+            elif k % 2 == 0:
+                nc.vector.tensor_scalar_mul(weights[k][:], probs[k][:], inv[:])
             else:
-                nc.gpsimd.tensor_scalar(weights[:], probs[k][:], inv[:], GAIN, ALU.mult, ALU.mult)
+                nc.scalar.activation(weights[k][:], probs[k][:], ACT.Copy, scale=inv[:])
+
+        sum_tags = (("bank4",), ("bank5",), ("bank0",), ("bank1", "bank2"))
+
+        def turn(k):
+            grp, r = divmod(k, PAIR)
+            blocks = BLOCKS // len(sum_tags[grp])
+            if r == 0:
+                sum_banks[grp] = [psum.tile([P, blocks, P], F32, name=f"sums_{tag}", tag=tag) for tag in sum_tags[grp]]
             for b in range(BLOCKS):
                 nc.tensor.matmul(
-                    sum_banks[grp][b // blocks][:, b % blocks, :], weights[:, b * P : (b + 1) * P], ident[:],
-                    start=(r == 0 and b % blocks == 0), stop=(r == n - 1 and b % blocks == blocks - 1),
+                    sum_banks[grp][b // blocks][:, b % blocks, :], weights[k][:, b * P : (b + 1) * P], ident[:],
+                    start=(r == 0 and b % blocks == 0), stop=(r == PAIR - 1 and b % blocks == blocks - 1),
                     is_transpose=True,
                 )
 
         def sum_heads(grp):
-            heads = GROUPS[grp] * P // ROWS
-            half, g0 = divmod(firsts[grp] * P // ROWS, HALF_HEADS)
+            half, g0 = divmod(grp * GROUP_HEADS, HALF_HEADS)
             by_block = head_sums[half][:, HALF_HEADS:].rearrange("p (b g) -> p b g", g=HALF_HEADS)
             blocks = BLOCKS // len(sum_banks[grp])
             for part, bank in enumerate(sum_banks[grp]):
                 nc.vector.tensor_reduce(
-                    by_block[:, part * blocks : (part + 1) * blocks, g0 : g0 + heads],
-                    bank[:].rearrange("p b (g j) -> p b g j", g=heads), AX.X, ALU.add,
+                    by_block[:, part * blocks : (part + 1) * blocks, g0 : g0 + GROUP_HEADS],
+                    bank[:].rearrange("p b (g j) -> p b g j", g=GROUP_HEADS), AX.X, ALU.add,
                 )
 
-        def smooth(half):
-            back = turn_pool.tile([P, 2 * P], F32, name="turn")
+        def smooth(half, copy, scale, tags):
+            back = psum.tile([P, 2 * P], F32, name=f"back{half}", tag=tags[0])
             for s in range(2):
-                nc.tensor.transpose(back[:, s * P : (s + 1) * P], head_sums[half][:, s * HALF_HEADS : s * HALF_HEADS + P], ident[:])
+                c0 = s * HALF_HEADS
+                nc.tensor.transpose(back[:, s * P : (s + 1) * P], head_sums[half][:, c0 : c0 + P], ident[:])
             reach = WINDOW - 1
             line = keep.tile([P, P + reach], F32, name=f"line{half}")
-            nc.scalar.copy(line[:], back[:, P - reach :])
-            forth = turn_pool.tile([P, P], F32, name="turn")
+            copy(line[:], back[:, P - reach :])
+            forth = psum.tile([P, P], F32, name=f"forth{half}", tag=tags[1])
             for s in range(WINDOW):
                 nc.tensor.matmul(
                     forth[:], line[:, s : s + P], ident[:], start=(s == 0), stop=(s == WINDOW - 1), is_transpose=True
                 )
             votes = keep.tile([P, BLOCKS, HALF_HEADS], F32, name=f"votes{half}")
-            nc.scalar.copy(votes[:].rearrange("p b g -> p (b g)"), forth[:])
+            scale(votes[:].rearrange("p b g -> p (b g)"), forth[:], GAIN)
             nc.sync.dma_start(
                 out[:, half * HALF_HEADS : (half + 1) * HALF_HEADS].rearrange("(b p) g -> p b g", p=P), votes[:]
             )
 
-        for step in range(len(tiles) + 2):
-            for batch in BATCHES[1:]:
-                if batch[0] == step + 2:
-                    quantise(batch)
-            if step < len(tiles):
+        for step in range(TILES + 2):
+            if step + 1 < GROUPS:
+                quantise(step + 1)
+            if step < TILES:
                 score(step)
-            if 0 <= step - 1 < len(tiles):
-                weigh(step - 1)
-            if step == 5:
-                sum_heads(0)
+            if 1 <= step <= TILES:
+                exponentiate(step - 1)
             if step == 7:
-                sum_heads(1)
-                smooth(0)
-            if 0 <= step - 2:
-                add_up(step - 2)
+                sum_heads(0)
+            if step >= 2:
+                normalise(step - 2)
+            for k in range(TILES):
+                if max(k + 2, (5, 6, 0, 0)[k // PAIR]) == step:
+                    turn(k)
+        sum_heads(1)
+        smooth(0, nc.scalar.copy, nc.scalar.mul, ("bank3", "bank4"))
         sum_heads(2)
-        smooth(1)
+        sum_heads(3)
+        smooth(1, nc.vector.tensor_copy, nc.vector.tensor_scalar_mul, ("bank6", "bank7"))

from contextlib import ExitStack

import concourse.mybir as mybir

D, T, I, Q, G = 512, 2048, 512, 1024, 64
FLOPS = 2 * D * I * Q

F32 = mybir.dt.float32
BF16 = mybir.dt.bfloat16
I32 = mybir.dt.int32
U32 = mybir.dt.uint32
U16 = mybir.dt.uint16
U8 = mybir.dt.uint8
FP8X4 = mybir.dt.float8_e4m3fn_x4
ACT = mybir.ActivationFunctionType
ALU = mybir.AluOpType
AX = mybir.AxisListType

P = 128
PACK = 4
RUN = 4
PAIR = 2
GROUP_ROWS = PAIR * P
GROUPS = Q // GROUP_ROWS
TILES = Q // P
GROUP_HEADS = G // GROUPS
BLOCKS = I // P
HALF_HEADS = G // 2
WINDOW = 5
GAIN = 102.4


def tile_attend_votes_kernel(tc, query, keys_words, keys_scales, offs, out):
    nc = tc.nc
    with ExitStack() as ctx:
        keep = ctx.enter_context(tc.tile_pool(name="keep", bufs=1))
        psum = ctx.enter_context(tc.psum_pool(name="psum", bufs=1))

        def load_group(grp):
            raw = keep.tile([P, PACK, GROUP_ROWS], F32, name=f"raw{grp}", tag=f"raw{grp}")
            rows = query[:, grp * GROUP_ROWS : (grp + 1) * GROUP_ROWS]
            nc.sync.dma_start(raw[:], rows.rearrange("(p t) q -> p t q", t=PACK))
            return raw

        offsets = keep.tile([P, I // 16], U16, name="offsets")
        pool_scales = keep.tile([P, T], U8, name="pool_scales", tag="scales_then_words", align_bytes=64)
        nc.gpsimd.memset(pool_scales[:].bitcast(I32), 0)
        raws = [load_group(0)]
        nc.sync.dma_start(offsets[:], offs)
        for quad in range(4):
            nc.sync.dma_start(
                pool_scales[32 * quad : 32 * quad + 4, :].bitcast(I32),
                keys_scales[0, 4 * quad : 4 * quad + 4, :].bitcast(I32),
            )
        head_sums = []
        for half, tag in enumerate(("pool_words", "raw1")):
            zeros = keep.tile([P, HALF_HEADS], F32, name=f"zeros{half}", tag=tag)
            nc.gpsimd.memset(zeros[:], 0.0)
            sums = keep.tile([P, (BLOCKS + 1) * HALF_HEADS], F32, name=f"head_sums{half}")
            nc.gpsimd.tensor_copy(sums[:, 0:HALF_HEADS], zeros[:])
            head_sums.append(sums)
        zero_square = keep.tile([P, P], F32, name="zero_square", tag="raw2")
        nc.gpsimd.memset(zero_square[:], 0.0)
        one_square = keep.tile([P, P], F32, name="one_square", tag="raw3")
        nc.scalar.activation(one_square[:], zero_square[:], ACT.Exp)
        ident = keep.tile([P, P], F32, name="ident")
        nc.gpsimd.affine_select(
            out=ident[:], in_=one_square[:], compare_op=ALU.is_equal, fill=0.0, base=0,
            pattern=[[-1, P]], channel_multiplier=1,
        )
        pool_words = keep.tile([P, T], U32, name="pool_words", tag="pool_words")
        nc.sync.dma_start(pool_words[:].bitcast(I32), keys_words[0].rearrange("p n t -> p (n t)").bitcast(I32))
        for grp in range(1, GROUPS):
            raws.append(load_group(grp))

        operands = {}
        scores = {}
        totals = {}
        probs = {}
        weights = {}
        sum_banks = {}

        def quantise(grp):
            woven = keep.tile([P, GROUP_ROWS * PACK], BF16, name=f"woven{grp}", tag=f"woven{grp}", align_bytes=64)
            src = raws[grp][:].rearrange("p t (u r j) -> p r u t j", r=PAIR, j=RUN)
            dst = woven[:].rearrange("p (r u j t) -> p r u t j", r=PAIR, j=RUN, t=PACK)
            if grp == 0:
                nc.vector.tensor_copy(dst[:, 0], src[:, 0])
                nc.scalar.copy(dst[:, 1], src[:, 1])
            elif grp % 2 == 0:
                nc.vector.tensor_copy(dst, src)
            else:
                nc.scalar.copy(dst, src)
            codes = keep.tile([P, GROUP_ROWS], U32, name=f"codes{grp}", align_bytes=64)
            scales = keep.tile([P, GROUP_ROWS], U8, name=f"scales{grp}", align_bytes=64)
            nc.vector.quantize_mx(out=codes[:].bitcast(FP8X4), scales=scales[:], in_=woven[:])
            operands[grp] = (codes, scales)

        quantise(0)
        key_scales = keep.tile([P, I], U8, name="key_scales", align_bytes=64)
        nc.vector.tensor_copy(key_scales[:], pool_scales[:].indirect(offsets[:]))
        key_words = keep.tile([P, I], U32, name="key_words", tag="scales_then_words", align_bytes=64)
        for h in range(2):
            nc.vector.tensor_copy(
                key_words[:, h * I // 2 : (h + 1) * I // 2],
                pool_words[:].indirect(offsets[:, h * I // 32 : (h + 1) * I // 32]),
            )

        def score(k):
            codes, scales = operands[k // PAIR]
            rows = slice(k % PAIR * P, (k % PAIR + 1) * P)
            scores[k] = psum.tile([P, I], F32, name=f"scores{k}", tag=f"bank{k}")
            cuts = 2 if k == 0 else 1
            for h in range(cuts):
                cols = slice(h * I // cuts, (h + 1) * I // cuts)
                nc.tensor.matmul_mx(
                    out=scores[k][:, cols], lhsT=codes[:, rows].bitcast(FP8X4), lhsT_scale=scales[:, rows],
                    rhs=key_words[:, cols].bitcast(FP8X4), rhs_scale=key_scales[:, cols], start=True, stop=True,
                )

        def exponentiate(k):
            tag = "woven1" if k == 1 else f"neg_max{k}"
            neg_max = keep.tile([P, 1], F32, name=f"neg_max{k}", tag=tag, align_bytes=64)
            nc.vector.tensor_reduce(neg_max[:], scores[k][:], AX.X, ALU.max, negate=True)
            probs[k] = keep.tile([P, I], F32, name=f"probs{k}")
            totals[k] = keep.tile([P, 1], F32, name=f"totals{k}")
            nc.scalar.activation(probs[k][:], scores[k][:], ACT.Exp, bias=neg_max[:], accum_out=totals[k][:])

        def normalise(k):
            inv = keep.tile([P, 1], F32, name=f"inv{k}")
            nc.vector.reciprocal(inv[:], totals[k][:])
            weights[k] = keep.tile([P, I], F32, name=f"weights{k}")
            if k < TILES // 2:
                nc.gpsimd.tensor_scalar(weights[k][:], probs[k][:], inv[:], 1.0, ALU.mult, ALU.mult)
            elif k == TILES - 1:
                nc.scalar.activation(weights[k][:, : I // 2], probs[k][:, : I // 2], ACT.Copy, scale=inv[:])
                nc.vector.tensor_scalar_mul(weights[k][:, I // 2 :], probs[k][:, I // 2 :], inv[:])
            elif k % 2 == 0:
                nc.vector.tensor_scalar_mul(weights[k][:], probs[k][:], inv[:])
            else:
                nc.scalar.activation(weights[k][:], probs[k][:], ACT.Copy, scale=inv[:])

        sum_tags = (("bank4",), ("bank5",), ("bank0",), ("bank1", "bank2"))

        def turn(k):
            grp, r = divmod(k, PAIR)
            blocks = BLOCKS // len(sum_tags[grp])
            if r == 0:
                sum_banks[grp] = [psum.tile([P, blocks, P], F32, name=f"sums_{tag}", tag=tag) for tag in sum_tags[grp]]
            for b in range(BLOCKS):
                nc.tensor.matmul(
                    sum_banks[grp][b // blocks][:, b % blocks, :], weights[k][:, b * P : (b + 1) * P], ident[:],
                    start=(r == 0 and b % blocks == 0), stop=(r == PAIR - 1 and b % blocks == blocks - 1),
                    is_transpose=True,
                )

        def sum_heads(grp):
            half, g0 = divmod(grp * GROUP_HEADS, HALF_HEADS)
            by_block = head_sums[half][:, HALF_HEADS:].rearrange("p (b g) -> p b g", g=HALF_HEADS)
            blocks = BLOCKS // len(sum_banks[grp])
            for part, bank in enumerate(sum_banks[grp]):
                nc.vector.tensor_reduce(
                    by_block[:, part * blocks : (part + 1) * blocks, g0 : g0 + GROUP_HEADS],
                    bank[:].rearrange("p b (g j) -> p b g j", g=GROUP_HEADS), AX.X, ALU.add,
                )

        def smooth(half, copy, scale, tags):
            back = psum.tile([P, 2 * P], F32, name=f"back{half}", tag=tags[0])
            for s in range(2):
                c0 = s * HALF_HEADS
                nc.tensor.transpose(back[:, s * P : (s + 1) * P], head_sums[half][:, c0 : c0 + P], ident[:])
            reach = WINDOW - 1
            line = keep.tile([P, P + reach], F32, name=f"line{half}")
            copy(line[:], back[:, P - reach :])
            forth = psum.tile([P, P], F32, name=f"forth{half}", tag=tags[1])
            for s in range(WINDOW):
                nc.tensor.matmul(
                    forth[:], line[:, s : s + P], ident[:], start=(s == 0), stop=(s == WINDOW - 1), is_transpose=True
                )
            votes = keep.tile([P, BLOCKS, HALF_HEADS], F32, name=f"votes{half}")
            scale(votes[:].rearrange("p b g -> p (b g)"), forth[:], GAIN)
            nc.sync.dma_start(
                out[:, half * HALF_HEADS : (half + 1) * HALF_HEADS].rearrange("(b p) g -> p b g", p=P), votes[:]
            )

        for step in range(TILES + 2):
            if step + 1 < GROUPS:
                quantise(step + 1)
            if step < TILES:
                score(step)
            if 1 <= step <= TILES:
                exponentiate(step - 1)
            if step == 7:
                sum_heads(0)
            if step >= 2:
                normalise(step - 2)
            for k in range(TILES):
                if max(k + 2, (5, 6, 0, 0)[k // PAIR]) == step:
                    turn(k)
        sum_heads(1)
        smooth(0, nc.scalar.copy, nc.scalar.mul, ("bank3", "bank4"))
        sum_heads(2)
        sum_heads(3)
        smooth(1, nc.vector.tensor_copy, nc.vector.tensor_scalar_mul, ("bank6", "bank7"))
